import numpy as np
CORES = [34,162,290,418,42,426]
N = 6
S, T = 4096, 1024
def entries(a): return a.T.reshape(-1)
def pack(v, P): return np.ascontiguousarray(np.asarray(v, np.int32).reshape(-1, P).T)
def lists(rng, how):
    M = rng.integers(0, S, (N, S)); b = rng.integers(0, S, T)
    if how == "alike": M = np.stack([rng.permutation(S) for f in range(N)]); b[:] = rng.integers(S)
    if how == "edge":
        M = np.where(rng.random((N, S)) < 0.5, 0, S - 1); w = rng.permutation(N) % 2 * (S - 1); M[:, 0] = w; M[:, S - 1] = S - 1 - w
        b = np.where(rng.random(T) < 0.5, 0, S - 1); b[rng.permutation(T)[:2]] = [0, S - 1]
    if how == "fold":
        V = np.stack([rng.permutation(S)[:4] for f in range(N + 1)]); M = V[np.arange(N)[:, None], rng.integers(0, 4, (N, S))]
        M[np.arange(N)[:, None], V[1:]] = V[:N]; b[rng.permutation(T)[:4]] = V[N]
    if how == "mixed":
        k = np.concatenate([[3, 3], rng.permutation(np.arange(N - 2) % 3)])
        for f in range(N): M[f] = [np.arange(S), rng.permutation(S), M[f], rng.integers(0, S, 4)[rng.integers(0, 4, S)]][k[f]]
    if how == "turn": M = np.stack([rng.permutation(S) for f in range(N)]); b = rng.permutation(S)[:T]
    return {"bp": np.stack([pack(m, 16) for m in M]), "st": np.broadcast_to(pack(b, 16), (N, 16, T // 16)).copy()}
def setup_inputs(rng):
    return dict({"tab": rng.standard_normal((N, 128, S), dtype=np.float32)}, **lists(rng, "uniform"))
def setup_inputs_alike(rng):
    d = setup_inputs(rng); d.update(lists(rng, "alike"))
    for k in ("tab",): d[k] = (d[k].astype(np.float32) * 1048576.0).astype(d[k].dtype)
    return d
def setup_inputs_edge(rng):
    d = setup_inputs(rng); d.update(lists(rng, "edge"))
    for k in ("tab",): d[k] = (d[k].astype(np.float32) * (1 / 1024.0)).astype(d[k].dtype)
    return d
def setup_inputs_fold(rng):
    d = setup_inputs(rng); d.update(lists(rng, "fold"))
    return d
def setup_inputs_mixed(rng):
    d = setup_inputs(rng); d.update(lists(rng, "mixed"))
    return d
def setup_inputs_turn(rng):
    d = setup_inputs(rng); d.update(lists(rng, "turn"))
    return d
def check_inputs(x):
    bad = []
    if x["bp"].min() < 0 or x["bp"].max() >= S: bad.append("bp out of range")
    if x["st"].min() < 0 or x["st"].max() >= S: bad.append("st out of range")
    if not all(np.array_equal(a, x["st"][0]) for a in x["st"]): bad.append("st isn't alike on all ranks")
    return bad
def reference(tab, bp, st):
    b = entries(st[0]); y = np.zeros((N, 128, T), tab.dtype)
    for f in range(N - 1, -1, -1):
        y[f] = tab[f][:, b]
        b = entries(bp[f])[b]
    return {"y": y}

@@ -1,0 +1,283 @@
+from concourse.bass import DstId, RemoteDMATransfer
+from concourse.mybir import AluOpType, ActivationFunctionType
+
+SCRATCH = {
+    "tabs": ("sbuf", [128, 4096], "float32"),
+    "wa": ("sbuf", [128, 4096], "float32"),
+    "wb": ("sbuf", [128, 4096], "float32"),
+    "w5": ("sbuf", [128, 4096], "int32"),
+    "ysb": ("sbuf", [128, 1024], "float32"),
+    "raw": ("sbuf", [128, 64], "int32"),
+    "x1": ("sbuf", [128, 32], "float32"),
+    "nat": ("sbuf", [128, 32], "float32"),
+    "stw": ("sbuf", [128, 8], "int32"),
+    "sa": ("sbuf", [128, 8], "int32"),
+    "sto": ("sbuf", [128, 64], "int32"),
+    "lin": ("sbuf", [128, 8], "uint16"),
+    "lst": ("sbuf", [128, 8], "uint16"),
+    "offs": ("sbuf", [128, 64], "uint16"),
+    "offx": ("sbuf", [128, 64], "uint16"),
+    "xr": ("sbuf", [128, 128], "float16"),
+    "xt": ("sbuf", [128, 128], "float16"),
+    "ones": ("sbuf", [128, 64], "float32"),
+    "sel": ("sbuf", [128, 64], "float32"),
+    "mk": ("sbuf", [128, 64], "float32"),
+    "bi": ("sbuf", [128, 128], "int32"),
+    "sel16": ("sbuf", [128, 64], "float16"),
+    "bt": ("sbuf", [128, 128], "float16"),
+    "ex": ("sbuf", [128, 64], "float16"),
+    "ps1": ("psum", [128, 64], "float32"),
+    "ps2": ("psum", [128, 64], "float32"),
+    "m1": ("dram", [128, 32], "float32"),
+    "m2": ("dram", [128, 32], "float32"),
+    "m3": ("dram", [128, 32], "float32"),
+    "m4": ("dram", [128, 32], "float32"),
+}
+SEMAPHORES = ["bpl", "stl", "sol", "tabl", "on", "ms1", "ms2", "ms3", "ssa", "gi", "gq", "vq", "pq", "sc", "sent", "sent2",
+              "m1a", "m2a", "m3a", "m4a", "lina", "offa", "wal", "wbl", "stq"]
+
+STEPS = {0: [(4, "wa", 0), (3, "wa", 1), (2, "wb", 0), (1, "wb", 1)],
+         1: [(4, "wa", 0), (3, "wb", 0), (2, "wa", 1)],
+         2: [(3, "wa", 0)], 3: [(4, "wa", 0)], 4: [], 5: [(5, "w5", 0)]}
+SWAPS = {0: 1, 1: 1, 2: 2, 3: 1, 5: 0}
+TAB = {0: [4096], 1: [3072, 1024], 2: [2048, 2048], 3: [2560, 1536], 4: [2048, 2048], 5: [1024, 1024, 2048]}
+
+
+def _helper(T, topo, near, src, dst):
+    for c in range(topo.CORES_PER_HOST * topo.host(near), topo.CORES_PER_HOST * (topo.host(near) + 1)):
+        if topo.chip(c) == topo.chip(near) and topo.die(c) == topo.die(src) and T.rank_of(c) is None \
+                and topo.may_write(src, c) and topo.may_write(c, dst):
+            return c
+    return None
+
+
+def _send(g, T, topo, core, dsts, name, src, sem, local):
+    mask = topo.mask(core, dsts[0])
+    for d in dsts:
+        mask &= topo.mask(core, d)
+    ids = []
+    for d in dsts:
+        rid, pid = topo.addr(d, core)
+        ids.append(DstId(rid=rid, pnc=pid))
+    g.remote_dma_fused([RemoteDMATransfer(dst_ids=ids, dma_engine_mask=mask, remote_sem=T.sem[sem], srcs=[src],
+                                          dsts=[T[name][:] for d in dsts], alu_op=0)], local_sem=T.sem[local])
+    return bin(mask).count("1")
+
+
+def rank_program(g, core, T, topo):
+    rank = T.rank_of(core)
+    C = T.cores
+    h0 = _helper(T, topo, C[0], C[3], C[1])
+    h1 = _helper(T, topo, C[1], C[2], C[0])
+
+    def arr(src, dst):
+        return bin(topo.mask(src, dst)).count("1")
+
+    if core == h0:
+        g.wait_ge(T.sem.m3a, arr(C[3], core))
+        n = _send(g, T, topo, core, [C[1]], "m3", T.m3[:], "m3a", "sent")
+        g.wait_ge(T.sem.lina, arr(C[5], core))
+        n += _send(g, T, topo, core, [C[1]], "lin", T.lin[:], "lina", "sent")
+        g.wait_ge(T.sem.sent, n)
+        return
+    if core == h1:
+        g.wait_ge(T.sem.m2a, arr(C[2], core))
+        n = _send(g, T, topo, core, [C[0]], "m2", T.m2[:], "m2a", "sent")
+        g.wait_ge(T.sem.sent, n)
+        return
+    if rank is None:
+        return
+
+    A = AluOpType
+    V, S, Y = g.vector, g.scalar, g.sync
+    eng = arr(C[3], C[0])
+    steps = STEPS[rank]
+    maps_in = [m for m, w, s in steps] if rank != 5 else []
+    uses_a, uses_b = rank in (0, 1, 2, 3), rank in (0, 1)
+    vn, gn = [0], [0]
+
+    def v(ins):
+        ins.then_inc(T.sem.vq, 1)
+        vn[0] += 1
+
+    def vw():
+        if vn[0]:
+            V.wait_ge(T.sem.vq, vn[0])
+
+    if 1 <= rank <= 4:
+        for a in range(4):
+            Y.dma_start(T.raw[32 * a:32 * a + 16, :], T.bp[:, 64 * a:64 * a + 64]).then_inc(T.sem.bpl, 16)
+            S.dma_start(T.raw[32 * a + 16:32 * a + 32, 0:63], T.bp[:, 64 * a + 1:64 * a + 64]).then_inc(T.sem.bpl, 16)
+    if rank == 5:
+        for q in range(8):
+            S.dma_start(T.stw[16 * q:16 * q + 16, :], T.st[:, 8 * q:8 * q + 8]).then_inc(T.sem.stl, 16)
+    pieces, c0 = [], 0
+    for w in TAB[rank]:
+        pieces.append((c0, c0 + w))
+        c0 += w
+
+    def load_tab(k):
+        lo, hi = pieces[k]
+        Y.dma_start(T.tabs[:, lo:hi], T.tab[:, lo:hi]).then_inc(T.sem.tabl, 16)
+    load_tab(0)
+
+    if rank != 4:
+        V.memset(T.ones[:], 1.0).then_inc(T.sem.on, 1)
+    if uses_a:
+        V.memset(T.wa[:, 0:1024], 0.0).then_inc(T.sem.ms1, 1)
+        V.memset(T.wa[:, 1024:2048], 0.0).then_inc(T.sem.ms2, 1)
+        S.wait_ge(T.sem.ms1, 1)
+        for k in (2, 3):
+            S.activation(T.wa[:, 1024 * k:1024 * k + 1024], T.wa[:, 0:1024], ActivationFunctionType.Copy).then_inc(T.sem.ssa, 1)
+    if rank == 5:
+        V.memset(T.w5[:, 0:2688], 0).then_inc(T.sem.ms1, 1)
+        g.iota(T.w5[:, 2688:4096], [[0, 1408]], 0, 0).then_inc(T.sem.gi, 1)
+    if 1 <= rank <= 4:
+        V.wait_ge(T.sem.bpl, 128)
+        v(V.tensor_copy(T.x1[:], T.raw[:, 0:63:2]))
+        vw()
+        v(V.transpose(T.nat[:], T.x1[:]))
+        g.wait_ge(T.sem.vq, vn[0])
+        dsts = {4: [C[0], C[3], C[1]], 3: [h0, C[0], C[2]], 2: [h1, C[1]], 1: [C[0]]}[rank]
+        nsent = _send(g, T, topo, core, dsts, "m%d" % rank, T.nat[:], "m%da" % rank, "sent")
+    if uses_b:
+        V.memset(T.wb[:], 0.0).then_inc(T.sem.ms3, 1)
+    if rank == 5:
+        V.wait_ge(T.sem.stl, 128)
+        v(V.tensor_scalar(T.sa[:], T.stw[:], 15, None, A.bitwise_and))
+        vw()
+        v(V.tensor_scalar(T.sa[:], T.sa[:], 4095, None, A.mult))
+        vw()
+        v(V.tensor_tensor(T.sa[:], T.sa[:], T.stw[:], A.add))
+        vw()
+        v(V.tensor_scalar(T.lin[:], T.sa[:], 0.0625, None, A.mult))
+
+    if rank != 4:
+        slot = steps[-1][2]
+        swapped = (SWAPS[rank] + len(steps) - 1) % 2
+
+        def gc(ins):
+            ins.then_inc(T.sem.gq, 1)
+            gn[0] += 1
+        g.wait_ge(T.sem.on, 1)
+        gc(g.iota(T.bi[:], [[1, 128]], 128, -1))
+        parts = [(T.sel[:], T.mk[:], T.ones[:], slot, [[16, 8], [0, 8]], [[0, 8], [16, 8]])]
+        if swapped:
+            parts = [(T.sel[:, e::2], T.mk[:, e::2], T.ones[:, 0:32], slot + 16 * e, [[32, 4], [0, 2], [0, 4]],
+                      [[0, 4], [16, 2], [32, 4]]) for e in range(2)]
+        for sel, mk, one, base, gp, cp in parts:
+            gc(g.affine_select(sel, one, gp, A.is_equal, 0.0, base, -1))
+            gc(g.affine_select(mk, one, [[-s, n] for s, n in cp], A.is_ge, 0.0, 0, 1))
+        g.wait_ge(T.sem.gq, gn[0])
+        for sel, mk, one, base, gp, cp in parts:
+            gc(g.affine_select(mk, mk, cp, A.is_ge, 0.0, 15, -1))
+        V.wait_ge(T.sem.gq, gn[0])
+        v(V.tensor_scalar(T.bi[:], T.bi[:], 15, None, A.bitwise_and))
+        v(V.tensor_copy(T.sel16[:], T.sel[:]))
+        vw()
+        v(V.tensor_scalar(T.bt[:], T.bi[:], 0, None, A.is_equal))
+
+    def windows(name):
+        todo = [(m, s) for m, w, s in steps if w == name]
+        for q, lo in ((Y, 0), (S, 4)):
+            if name == "wa":
+                q.wait_ge(T.sem.ms1, 1)
+                q.wait_ge(T.sem.ms2, 1)
+                q.wait_ge(T.sem.ssa, 2)
+            if name == "wb":
+                q.wait_ge(T.sem.ms3, 1)
+            if name == "w5":
+                q.wait_ge(T.sem.ms1, 1)
+                q.wait_ge(T.sem.gi, 1)
+            for m, s in todo:
+                if name != "w5":
+                    q.wait_ge(T.sem["m%da" % m], eng)
+                src = T.bp[:] if name == "w5" else T["m%d" % m][:]
+                sem = {"wa": "wal", "wb": "wbl", "w5": "bpl"}[name]
+                for gr in range(lo, lo + 4):
+                    p = 16 * gr + s
+                    q.dma_start(T[name][p:p + 1, :], src).then_inc(T.sem[sem], 16)
+        return 128 * len(todo)
+
+    need = {}
+    if rank == 5:
+        need["w5"] = ("bpl", windows("w5"))
+        load_tab(1)
+        for q in range(8):
+            S.dma_start(T.sto[16 * q:16 * q + 16, :], T.st[:]).then_inc(T.sem.sol, 16)
+        Y.wait_ge(T.sem.sent, eng)
+        load_tab(2)
+    elif rank == 0:
+        need["wa"] = ("wal", windows("wa"))
+        need["wb"] = ("wbl", windows("wb"))
+    elif rank == 3:
+        need["wa"] = ("wal", windows("wa"))
+        Y.wait_ge(T.sem.sent, nsent)
+        load_tab(1)
+    else:
+        Y.wait_ge(T.sem.sent, nsent)
+        load_tab(1)
+        if uses_a:
+            need["wa"] = ("wal", windows("wa"))
+        if uses_b:
+            need["wb"] = ("wbl", windows("wb"))
+
+    if rank == 4:
+        V.wait_ge(T.sem.offa, eng)
+        S.wait_ge(T.sem.offa, eng)
+    else:
+        cur = T.lin
+        if rank != 5:
+            V.wait_ge(T.sem.lina, eng)
+        ready = []
+        for k, (m, w, s) in enumerate(steps):
+            if w not in ready:
+                V.wait_ge(T.sem[need[w][0]], need[w][1])
+                ready.append(w)
+            vw()
+            v(V.tensor_scalar(T.xr[:], T[w][:, 0:4096].indirect(cur[:, 0:8]), 2048.0, None, A.subtract))
+            x_at = vn[0]
+            last = k == len(steps) - 1
+            if not last or rank in (3, 5):
+                vw()
+                v(V.transpose(T.xt[:], T.xr[:]))
+                vw()
+                v(V.tensor_scalar(T.lst[:], T.xt[:, s::16], 2048.0, None, A.add))
+                cur = T.lst
+                l_at = vn[0]
+        if rank == 3:
+            g.wait_ge(T.sem.vq, l_at)
+            n2 = _send(g, T, topo, core, [C[2]], "lin", T.lst[:], "lina", "sent2")
+        if rank == 5:
+            g.wait_ge(T.sem.vq, l_at)
+            nsent = _send(g, T, topo, core, [C[0], h0, C[3]], "lin", T.lst[:], "lina", "sent")
+        out = T.offx if rank == 5 else T.offs
+        g.tensor.wait_ge(T.sem.vq, x_at)
+        g.tensor.matmul(T.ps1[:], T.xr[:], T.sel16[:], True, True).then_inc(T.sem.pq, 1)
+        V.wait_ge(T.sem.pq, 1)
+        v(V.tensor_tensor(T.ex[:], T.ps1[:], T.mk[:], A.mult))
+        g.tensor.wait_ge(T.sem.vq, vn[0])
+        g.tensor.matmul(T.ps2[:], T.bt[:], T.ex[:], True, True).then_inc(T.sem.pq, 1)
+        V.wait_ge(T.sem.pq, 2)
+        v(V.tensor_scalar(out[:], T.ps2[:], 2048.0, None, A.add))
+        if rank == 5:
+            g.wait_ge(T.sem.vq, vn[0])
+            n2 = _send(g, T, topo, core, [C[4]], "offs", T.offx[:], "offa", "sent2")
+            V.wait_ge(T.sem.sol, 128)
+            v(V.tensor_copy(T.offs[:], T.sto[:]))
+        vw()
+        S.wait_ge(T.sem.vq, vn[0])
+
+    V.wait_ge(T.sem.tabl, 16 * len(pieces))
+    v(V.tensor_copy(T.ysb[:, 0:512], T.tabs[:, 0:4096].indirect(T.offs[:, 0:32])))
+    S.wait_ge(T.sem.tabl, 16 * len(pieces))
+    S.activation(T.ysb[:, 512:1024], T.tabs[:, 0:4096].indirect(T.offs[:, 32:64]), ActivationFunctionType.Copy).then_inc(T.sem.sc, 1)
+    Y.wait_ge(T.sem.vq, vn[0])
+    Y.dma_start(T.y[:, 0:512], T.ysb[:, 0:512]).then_inc(T.sem.stq, 16)
+    S.wait_ge(T.sem.sc, 1)
+    S.dma_start(T.y[:, 512:1024], T.ysb[:, 512:1024]).then_inc(T.sem.stq, 16)
+    Y.wait_ge(T.sem.stq, 32)
+    if rank in (1, 2, 3, 4, 5):
+        g.wait_ge(T.sem.sent, nsent)
+    if rank in (3, 5):
+        g.wait_ge(T.sem.sent2, n2)

@@ -34,21 +34,13 @@ SCRATCH = {
     "m4": ("dram", [128, 32], "float32"),
 }
 SEMAPHORES = ["bpl", "stl", "sol", "tabl", "on", "ms1", "ms2", "ms3", "ssa", "gi", "gq", "vq", "pq", "sc", "sent", "sent2",
-              "m1a", "m2a", "m3a", "m4a", "lina", "offa", "wal", "wbl", "stq"]
+              "sent3", "w5l", "m1a", "m2a", "m3a", "m4a", "lina", "offa", "wal", "wbl", "stq"]
 
 STEPS = {0: [(4, "wa", 0), (3, "wa", 1), (2, "wb", 0), (1, "wb", 1)],
          1: [(4, "wa", 0), (3, "wb", 0), (2, "wa", 1)],
          2: [(3, "wa", 0)], 3: [(4, "wa", 0)], 4: [], 5: [(5, "w5", 0)]}
 SWAPS = {0: 1, 1: 1, 2: 2, 3: 1, 5: 0}
-TAB = {0: [4096], 1: [3072, 1024], 2: [2048, 2048], 3: [2560, 1536], 4: [2048, 2048], 5: [1024, 1024, 2048]}
-
-
-def _helper(T, topo, near, src, dst):
-    for c in range(topo.CORES_PER_HOST * topo.host(near), topo.CORES_PER_HOST * (topo.host(near) + 1)):
-        if topo.chip(c) == topo.chip(near) and topo.die(c) == topo.die(src) and T.rank_of(c) is None \
-                and topo.may_write(src, c) and topo.may_write(c, dst):
-            return c
-    return None
+TAB = {0: [4096], 1: [3072, 1024], 2: [3072, 1024], 3: [3072, 1024], 4: [3072, 1024], 5: [1536, 1536, 1024]}
 
 
 def _send(g, T, topo, core, dsts, name, src, sem, local):
@@ -66,33 +58,13 @@ def _send(g, T, topo, core, dsts, name, src, sem, local):
 
 def rank_program(g, core, T, topo):
     rank = T.rank_of(core)
-    C = T.cores
-    h0 = _helper(T, topo, C[0], C[3], C[1])
-    h1 = _helper(T, topo, C[1], C[2], C[0])
-
-    def arr(src, dst):
-        return bin(topo.mask(src, dst)).count("1")
-
-    if core == h0:
-        g.wait_ge(T.sem.m3a, arr(C[3], core))
-        n = _send(g, T, topo, core, [C[1]], "m3", T.m3[:], "m3a", "sent")
-        g.wait_ge(T.sem.lina, arr(C[5], core))
-        n += _send(g, T, topo, core, [C[1]], "lin", T.lin[:], "lina", "sent")
-        g.wait_ge(T.sem.sent, n)
-        return
-    if core == h1:
-        g.wait_ge(T.sem.m2a, arr(C[2], core))
-        n = _send(g, T, topo, core, [C[0]], "m2", T.m2[:], "m2a", "sent")
-        g.wait_ge(T.sem.sent, n)
-        return
     if rank is None:
         return
-
+    C = T.cores
     A = AluOpType
     V, S, Y = g.vector, g.scalar, g.sync
-    eng = arr(C[3], C[0])
+    eng = bin(topo.mask(C[3], C[0])).count("1")
     steps = STEPS[rank]
-    maps_in = [m for m, w, s in steps] if rank != 5 else []
     uses_a, uses_b = rank in (0, 1, 2, 3), rank in (0, 1)
     vn, gn = [0], [0]
 
@@ -110,7 +82,7 @@ def rank_program(g, core, T, topo):
             S.dma_start(T.raw[32 * a + 16:32 * a + 32, 0:63], T.bp[:, 64 * a + 1:64 * a + 64]).then_inc(T.sem.bpl, 16)
     if rank == 5:
         for q in range(8):
-            S.dma_start(T.stw[16 * q:16 * q + 16, :], T.st[:, 8 * q:8 * q + 8]).then_inc(T.sem.stl, 16)
+            (Y if q % 2 else S).dma_start(T.stw[16 * q:16 * q + 16, :], T.st[:, 8 * q:8 * q + 8]).then_inc(T.sem.stl, 16)
     pieces, c0 = [], 0
     for w in TAB[rank]:
         pieces.append((c0, c0 + w))
@@ -121,38 +93,7 @@ def rank_program(g, core, T, topo):
         Y.dma_start(T.tabs[:, lo:hi], T.tab[:, lo:hi]).then_inc(T.sem.tabl, 16)
     load_tab(0)
 
-    if rank != 4:
-        V.memset(T.ones[:], 1.0).then_inc(T.sem.on, 1)
-    if uses_a:
-        V.memset(T.wa[:, 0:1024], 0.0).then_inc(T.sem.ms1, 1)
-        V.memset(T.wa[:, 1024:2048], 0.0).then_inc(T.sem.ms2, 1)
-        S.wait_ge(T.sem.ms1, 1)
-        for k in (2, 3):
-            S.activation(T.wa[:, 1024 * k:1024 * k + 1024], T.wa[:, 0:1024], ActivationFunctionType.Copy).then_inc(T.sem.ssa, 1)
-    if rank == 5:
-        V.memset(T.w5[:, 0:2688], 0).then_inc(T.sem.ms1, 1)
-        g.iota(T.w5[:, 2688:4096], [[0, 1408]], 0, 0).then_inc(T.sem.gi, 1)
-    if 1 <= rank <= 4:
-        V.wait_ge(T.sem.bpl, 128)
-        v(V.tensor_copy(T.x1[:], T.raw[:, 0:63:2]))
-        vw()
-        v(V.transpose(T.nat[:], T.x1[:]))
-        g.wait_ge(T.sem.vq, vn[0])
-        dsts = {4: [C[0], C[3], C[1]], 3: [h0, C[0], C[2]], 2: [h1, C[1]], 1: [C[0]]}[rank]
-        nsent = _send(g, T, topo, core, dsts, "m%d" % rank, T.nat[:], "m%da" % rank, "sent")
-    if uses_b:
-        V.memset(T.wb[:], 0.0).then_inc(T.sem.ms3, 1)
-    if rank == 5:
-        V.wait_ge(T.sem.stl, 128)
-        v(V.tensor_scalar(T.sa[:], T.stw[:], 15, None, A.bitwise_and))
-        vw()
-        v(V.tensor_scalar(T.sa[:], T.sa[:], 4095, None, A.mult))
-        vw()
-        v(V.tensor_tensor(T.sa[:], T.sa[:], T.stw[:], A.add))
-        vw()
-        v(V.tensor_scalar(T.lin[:], T.sa[:], 0.0625, None, A.mult))
-
-    if rank != 4:
+    def consts_g():
         slot = steps[-1][2]
         swapped = (SWAPS[rank] + len(steps) - 1) % 2
 
@@ -171,14 +112,61 @@ def rank_program(g, core, T, topo):
         g.wait_ge(T.sem.gq, gn[0])
         for sel, mk, one, base, gp, cp in parts:
             gc(g.affine_select(mk, mk, cp, A.is_ge, 0.0, 15, -1))
+
+    def consts_v():
         V.wait_ge(T.sem.gq, gn[0])
         v(V.tensor_scalar(T.bi[:], T.bi[:], 15, None, A.bitwise_and))
         v(V.tensor_copy(T.sel16[:], T.sel[:]))
         vw()
         v(V.tensor_scalar(T.bt[:], T.bi[:], 0, None, A.is_equal))
 
+    if rank != 4:
+        V.memset(T.ones[:], 1.0).then_inc(T.sem.on, 1)
+    if rank in (0, 1, 2, 3):
+        consts_g()
+    if uses_a:
+        V.memset(T.wa[:, 0:1024], 0.0).then_inc(T.sem.ms1, 1)
+        V.memset(T.wa[:, 1024:2048], 0.0).then_inc(T.sem.ms2, 1)
+        S.wait_ge(T.sem.ms1, 1)
+        for k in (2, 3):
+            S.activation(T.wa[:, 1024 * k:1024 * k + 1024], T.wa[:, 0:1024], ActivationFunctionType.Copy).then_inc(T.sem.ssa, 1)
+    if rank == 5:
+        V.memset(T.w5[:, 0:2688], 0).then_inc(T.sem.ms1, 1)
+        g.iota(T.w5[:, 2688:4096], [[0, 1408]], 0, 0).then_inc(T.sem.gi, 1)
+    nsent, n2 = 0, 0
+    if 1 <= rank <= 4:
+        V.wait_ge(T.sem.bpl, 128)
+        v(V.tensor_copy(T.x1[:], T.raw[:, 0:63:2]))
+        vw()
+        v(V.transpose(T.nat[:], T.x1[:]))
+        g.wait_ge(T.sem.vq, vn[0])
+        for dsts in {4: [[C[0], C[3]], [C[1]]], 3: [[C[2], C[0]]], 2: [[C[1]]], 1: [[C[0]]]}[rank]:
+            nsent += _send(g, T, topo, core, dsts, "m%d" % rank, T.nat[:], "m%da" % rank, "sent")
+    if rank in (1, 2):
+        m, to = {1: (2, C[0]), 2: (3, C[1])}[rank]
+        g.wait_ge(T.sem["m%da" % m], eng)
+        n2 = _send(g, T, topo, core, [to], "m%d" % m, T["m%d" % m][:], "m%da" % m, "sent2")
+    if rank == 4:
+        g.wait_ge(T.sem.lina, eng)
+        n2 = _send(g, T, topo, core, [C[1]], "lin", T.lin[:], "lina", "sent2")
+    if rank in (0, 1, 2, 3):
+        consts_v()
+    if uses_b:
+        V.memset(T.wb[:], 0.0).then_inc(T.sem.ms3, 1)
+    if rank == 5:
+        V.wait_ge(T.sem.stl, 128)
+        v(V.tensor_scalar(T.sa[:], T.stw[:], 15, None, A.bitwise_and))
+        vw()
+        v(V.tensor_scalar(T.sa[:], T.sa[:], 4095, None, A.mult))
+        vw()
+        v(V.tensor_tensor(T.sa[:], T.sa[:], T.stw[:], A.add))
+        vw()
+        v(V.tensor_scalar(T.lin[:], T.sa[:], 0.0625, None, A.mult))
+
     def windows(name):
-        todo = [(m, s) for m, w, s in steps if w == name]
+        todo = sorted((m, s) for m, w, s in steps if w == name)
+        if rank == 0 and name == "wa":
+            todo = todo[::-1]
         for q, lo in ((Y, 0), (S, 4)):
             if name == "wa":
                 q.wait_ge(T.sem.ms1, 1)
@@ -193,19 +181,18 @@ def rank_program(g, core, T, topo):
                 if name != "w5":
                     q.wait_ge(T.sem["m%da" % m], eng)
                 src = T.bp[:] if name == "w5" else T["m%d" % m][:]
-                sem = {"wa": "wal", "wb": "wbl", "w5": "bpl"}[name]
                 for gr in range(lo, lo + 4):
                     p = 16 * gr + s
-                    q.dma_start(T[name][p:p + 1, :], src).then_inc(T.sem[sem], 16)
+                    q.dma_start(T[name][p:p + 1, :], src).then_inc(T.sem[name + "l"], 16)
         return 128 * len(todo)
 
     need = {}
     if rank == 5:
-        need["w5"] = ("bpl", windows("w5"))
+        need["w5"] = ("w5l", windows("w5"))
         load_tab(1)
         for q in range(8):
             S.dma_start(T.sto[16 * q:16 * q + 16, :], T.st[:]).then_inc(T.sem.sol, 16)
-        Y.wait_ge(T.sem.sent, eng)
+        Y.wait_ge(T.sem.sent2, eng)
         load_tab(2)
     elif rank == 0:
         need["wa"] = ("wal", windows("wa"))
@@ -237,8 +224,7 @@ def rank_program(g, core, T, topo):
             vw()
             v(V.tensor_scalar(T.xr[:], T[w][:, 0:4096].indirect(cur[:, 0:8]), 2048.0, None, A.subtract))
             x_at = vn[0]
-            last = k == len(steps) - 1
-            if not last or rank in (3, 5):
+            if k < len(steps) - 1 or rank in (3, 5):
                 vw()
                 v(V.transpose(T.xt[:], T.xr[:]))
                 vw()
@@ -250,7 +236,10 @@ def rank_program(g, core, T, topo):
             n2 = _send(g, T, topo, core, [C[2]], "lin", T.lst[:], "lina", "sent2")
         if rank == 5:
             g.wait_ge(T.sem.vq, l_at)
-            nsent = _send(g, T, topo, core, [C[0], h0, C[3]], "lin", T.lst[:], "lina", "sent")
+            n2 = _send(g, T, topo, core, [C[4], C[3], C[0]], "lin", T.lst[:], "lina", "sent2")
+            consts_g()
+            consts_v()
+            x_at = vn[0]
         out = T.offx if rank == 5 else T.offs
         g.tensor.wait_ge(T.sem.vq, x_at)
         g.tensor.matmul(T.ps1[:], T.xr[:], T.sel16[:], True, True).then_inc(T.sem.pq, 1)
@@ -262,7 +251,7 @@ def rank_program(g, core, T, topo):
         v(V.tensor_scalar(out[:], T.ps2[:], 2048.0, None, A.add))
         if rank == 5:
             g.wait_ge(T.sem.vq, vn[0])
-            n2 = _send(g, T, topo, core, [C[4]], "offs", T.offx[:], "offa", "sent2")
+            n3 = _send(g, T, topo, core, [C[4]], "offs", T.offx[:], "offa", "sent3")
             V.wait_ge(T.sem.sol, 128)
             v(V.tensor_copy(T.offs[:], T.sto[:]))
         vw()
@@ -277,7 +266,11 @@ def rank_program(g, core, T, topo):
     S.wait_ge(T.sem.sc, 1)
     S.dma_start(T.y[:, 512:1024], T.ysb[:, 512:1024]).then_inc(T.sem.stq, 16)
     Y.wait_ge(T.sem.stq, 32)
-    if rank in (1, 2, 3, 4, 5):
+    if 1 <= rank <= 4:
         g.wait_ge(T.sem.sent, nsent)
-    if rank in (3, 5):
+    if rank >= 2:
         g.wait_ge(T.sem.sent2, n2)
+    if rank == 1:
+        g.wait_ge(T.sem.sent2, n2)
+    if rank == 5:
+        g.wait_ge(T.sem.sent3, n3)

@@ -5,26 +5,34 @@ SCRATCH = {
     "tabs": ("sbuf", [128, 4096], "float32"),
     "wa": ("sbuf", [128, 4096], "float32"),
     "wb": ("sbuf", [128, 4096], "float32"),
-    "w5": ("sbuf", [128, 4096], "int32"),
+    "w5": ("sbuf", [128, 256], "int32"),
     "ysb": ("sbuf", [128, 1024], "float32"),
     "raw": ("sbuf", [128, 64], "int32"),
     "x1": ("sbuf", [128, 32], "float32"),
     "nat": ("sbuf", [128, 32], "float32"),
     "stw": ("sbuf", [128, 8], "int32"),
     "sa": ("sbuf", [128, 8], "int32"),
+    "sb": ("sbuf", [128, 8], "int32"),
+    "lo": ("sbuf", [128, 8], "uint16"),
+    "hi": ("sbuf", [128, 8], "uint16"),
+    "i16": ("sbuf", [128, 16], "float32"),
+    "mrow": ("sbuf", [128, 128], "float32"),
+    "xm": ("sbuf", [128, 128], "float32"),
+    "gs": ("sbuf", [128, 8], "float32"),
     "sto": ("sbuf", [128, 64], "int32"),
     "lin": ("sbuf", [128, 8], "uint16"),
     "lst": ("sbuf", [128, 8], "uint16"),
+    "l16": ("sbuf", [128, 8], "float16"),
     "offs": ("sbuf", [128, 64], "uint16"),
-    "offx": ("sbuf", [128, 64], "uint16"),
     "xr": ("sbuf", [128, 128], "float16"),
     "xt": ("sbuf", [128, 128], "float16"),
     "ones": ("sbuf", [128, 64], "float32"),
     "sel": ("sbuf", [128, 64], "float32"),
     "mk": ("sbuf", [128, 64], "float32"),
-    "bi": ("sbuf", [128, 128], "int32"),
+    "bi": ("sbuf", [128, 16], "int32"),
     "sel16": ("sbuf", [128, 64], "float16"),
     "bt": ("sbuf", [128, 128], "float16"),
+    "bg": ("sbuf", [128, 1024], "float16"),
     "ex": ("sbuf", [128, 64], "float16"),
     "ps1": ("psum", [128, 64], "float32"),
     "ps2": ("psum", [128, 64], "float32"),
@@ -33,14 +41,14 @@ SCRATCH = {
     "m3": ("dram", [128, 32], "float32"),
     "m4": ("dram", [128, 32], "float32"),
 }
-SEMAPHORES = ["bpl", "stl", "sol", "tabl", "on", "ms1", "ms2", "ms3", "ssa", "gi", "gq", "vq", "pq", "sc", "sent", "sent2",
-              "sent3", "w5l", "m1a", "m2a", "m3a", "m4a", "lina", "offa", "wal", "wbl", "stq"]
+SEMAPHORES = ["bpl", "stl", "sol", "tabl", "on", "msa0", "msa1", "msb0", "msb1", "ssa", "ssb", "gq", "vq", "pq", "sc", "sent",
+              "sent2", "w5l", "m1a", "m2a", "m3a", "m4a", "lina", "wal", "wbl", "stq"]
 
 STEPS = {0: [(4, "wa", 0), (3, "wa", 1), (2, "wb", 0), (1, "wb", 1)],
          1: [(4, "wa", 0), (3, "wb", 0), (2, "wa", 1)],
-         2: [(3, "wa", 0)], 3: [(4, "wa", 0)], 4: [], 5: [(5, "w5", 0)]}
-SWAPS = {0: 1, 1: 1, 2: 2, 3: 1, 5: 0}
-TAB = {0: [4096], 1: [3072, 1024], 2: [3072, 1024], 3: [3072, 1024], 4: [3072, 1024], 5: [1536, 1536, 1024]}
+         2: [(3, "wa", 0)], 3: [(4, "wa", 0)], 4: [], 5: []}
+SWAPS = {0: 0, 1: 0, 2: 1, 3: 0}
+TAB = {0: [3584, 512], 1: [3072, 1024], 2: [2048, 576, 1472], 3: [2432, 1344, 320], 4: [2432, 896, 768], 5: [2176, 1920]}
 
 
 def _send(g, T, topo, core, dsts, name, src, sem, local):
@@ -62,11 +70,12 @@ def rank_program(g, core, T, topo):
         return
     C = T.cores
     A = AluOpType
+    COPY = ActivationFunctionType.Copy
     V, S, Y = g.vector, g.scalar, g.sync
     eng = bin(topo.mask(C[3], C[0])).count("1")
     steps = STEPS[rank]
-    uses_a, uses_b = rank in (0, 1, 2, 3), rank in (0, 1)
-    vn, gn = [0], [0]
+    uses_b = rank in (0, 1)
+    vn, gn, nt = [0], [0], [0]
 
     def v(ins):
         ins.then_inc(T.sem.vq, 1)
@@ -76,6 +85,17 @@ def rank_program(g, core, T, topo):
         if vn[0]:
             V.wait_ge(T.sem.vq, vn[0])
 
+    def gc(ins):
+        ins.then_inc(T.sem.gq, 1)
+        gn[0] += 1
+
+    def load_tab(q):
+        k = nt[0]
+        nt[0] += 1
+        a = sum(TAB[rank][:k])
+        b = a + TAB[rank][k]
+        q.dma_start(T.tabs[:, a:b], T.tab[:, a:b]).then_inc(T.sem.tabl, 16)
+
     if 1 <= rank <= 4:
         for a in range(4):
             Y.dma_start(T.raw[32 * a:32 * a + 16, :], T.bp[:, 64 * a:64 * a + 64]).then_inc(T.sem.bpl, 16)
@@ -83,56 +103,56 @@ def rank_program(g, core, T, topo):
     if rank == 5:
         for q in range(8):
             (Y if q % 2 else S).dma_start(T.stw[16 * q:16 * q + 16, :], T.st[:, 8 * q:8 * q + 8]).then_inc(T.sem.stl, 16)
-    pieces, c0 = [], 0
-    for w in TAB[rank]:
-        pieces.append((c0, c0 + w))
-        c0 += w
+        for q in range(8):
+            (Y if q % 2 else S).dma_start(T.w5[16 * q:16 * q + 16, :], T.bp[:]).then_inc(T.sem.w5l, 16)
+    load_tab(Y)
 
-    def load_tab(k):
-        lo, hi = pieces[k]
-        Y.dma_start(T.tabs[:, lo:hi], T.tab[:, lo:hi]).then_inc(T.sem.tabl, 16)
-    load_tab(0)
+    parts = []
+    if rank <= 3:
+        slot = steps[-1][2]
+        if (SWAPS[rank] + len(steps) - 1) % 2 == 0:
+            parts = [(T.sel[:], T.mk[:], T.ones[:], [[0, 8], [16, 8]], [[16, 8], [0, 8]], 0)]
+        else:
+            parts = [(T.sel[:, h::2], T.mk[:, h::2], T.ones[:, 0:32], [[0, 4], [16, 2], [32, 4]],
+                      [[32, 4], [0, 2], [0, 4]], 16 * h) for h in range(2)]
+
+    V.memset(T.ones[:], 1.0).then_inc(T.sem.on, 1)
+    g.wait_ge(T.sem.on, 1)
+    gc(g.iota(T.bi[:], [[1, 16]], 128, -1))
+    for sel, mk, one, gp, cp, base in parts:
+        gc(g.affine_select(sel, one, gp, A.is_equal, 0.0, slot, -1))
+        gc(g.affine_select(mk, one, [[-s, n] for s, n in cp], A.is_ge, 0.0, -base, 1))
+    if rank >= 4:
+        gc(g.affine_select(T.gs[:], T.ones[:, 0:8], [[-16, 8]], A.is_ge, 0.0, 0, 1))
+        g.wait_ge(T.sem.gq, gn[0])
+        gc(g.affine_select(T.gs[:], T.gs[:], [[16, 8]], A.is_ge, 0.0, 15, -1))
 
     def consts_g():
-        slot = steps[-1][2]
-        swapped = (SWAPS[rank] + len(steps) - 1) % 2
-
-        def gc(ins):
-            ins.then_inc(T.sem.gq, 1)
-            gn[0] += 1
-        g.wait_ge(T.sem.on, 1)
-        gc(g.iota(T.bi[:], [[1, 128]], 128, -1))
-        parts = [(T.sel[:], T.mk[:], T.ones[:], slot, [[16, 8], [0, 8]], [[0, 8], [16, 8]])]
-        if swapped:
-            parts = [(T.sel[:, e::2], T.mk[:, e::2], T.ones[:, 0:32], slot + 16 * e, [[32, 4], [0, 2], [0, 4]],
-                      [[0, 4], [16, 2], [32, 4]]) for e in range(2)]
-        for sel, mk, one, base, gp, cp in parts:
-            gc(g.affine_select(sel, one, gp, A.is_equal, 0.0, base, -1))
-            gc(g.affine_select(mk, one, [[-s, n] for s, n in cp], A.is_ge, 0.0, 0, 1))
-        g.wait_ge(T.sem.gq, gn[0])
-        for sel, mk, one, base, gp, cp in parts:
-            gc(g.affine_select(mk, mk, cp, A.is_ge, 0.0, 15, -1))
+        if parts:
+            g.wait_ge(T.sem.gq, gn[0])
+        for sel, mk, one, gp, cp, base in parts:
+            gc(g.affine_select(mk, mk, cp, A.is_ge, 0.0, base + 15, -1))
 
     def consts_v():
         V.wait_ge(T.sem.gq, gn[0])
         v(V.tensor_scalar(T.bi[:], T.bi[:], 15, None, A.bitwise_and))
-        v(V.tensor_copy(T.sel16[:], T.sel[:]))
+        if rank <= 3:
+            v(V.tensor_copy(T.sel16[:], T.sel[:]))
         vw()
-        v(V.tensor_scalar(T.bt[:], T.bi[:], 0, None, A.is_equal))
+        v(V.tensor_scalar(T.bt[:, 0:16], T.bi[:], 0, None, A.is_equal))
+        for w in (16, 32, 64):
+            vw()
+            v(V.tensor_copy(T.bt[:, w:2 * w], T.bt[:, 0:w]))
+        if rank == 4:
+            vw()
+            for G in range(8):
+                v(V.tensor_scalar(T.bg[:, 128 * G:128 * G + 128], T.bt[:], T.gs[:, G:G + 1], None, A.mult))
 
-    if rank != 4:
-        V.memset(T.ones[:], 1.0).then_inc(T.sem.on, 1)
-    if rank in (0, 1, 2, 3):
-        consts_g()
-    if uses_a:
-        V.memset(T.wa[:, 0:1024], 0.0).then_inc(T.sem.ms1, 1)
-        V.memset(T.wa[:, 1024:2048], 0.0).then_inc(T.sem.ms2, 1)
-        S.wait_ge(T.sem.ms1, 1)
+    if rank <= 3:
+        V.memset(T.wa[:, 0:1024], 0.0).then_inc(T.sem.msa0, 1)
+        S.wait_ge(T.sem.msa0, 1)
         for k in (2, 3):
-            S.activation(T.wa[:, 1024 * k:1024 * k + 1024], T.wa[:, 0:1024], ActivationFunctionType.Copy).then_inc(T.sem.ssa, 1)
-    if rank == 5:
-        V.memset(T.w5[:, 0:2688], 0).then_inc(T.sem.ms1, 1)
-        g.iota(T.w5[:, 2688:4096], [[0, 1408]], 0, 0).then_inc(T.sem.gi, 1)
+            S.activation(T.wa[:, 1024 * k:1024 * k + 1024], T.wa[:, 0:1024], COPY).then_inc(T.sem.ssa, 1)
     nsent, n2 = 0, 0
     if 1 <= rank <= 4:
         V.wait_ge(T.sem.bpl, 128)
@@ -140,8 +160,17 @@ def rank_program(g, core, T, topo):
         vw()
         v(V.transpose(T.nat[:], T.x1[:]))
         g.wait_ge(T.sem.vq, vn[0])
-        for dsts in {4: [[C[0], C[3]], [C[1]]], 3: [[C[2], C[0]]], 2: [[C[1]]], 1: [[C[0]]]}[rank]:
-            nsent += _send(g, T, topo, core, dsts, "m%d" % rank, T.nat[:], "m%da" % rank, "sent")
+        dsts = {4: [C[3], C[0], C[1]], 3: [C[2], C[0]], 2: [C[1]], 1: [C[0]]}[rank]
+        nsent = _send(g, T, topo, core, dsts, "m%d" % rank, T.nat[:], "m%da" % rank, "sent")
+    consts_g()
+    if rank <= 3:
+        V.memset(T.wa[:, 1024:2048], 0.0).then_inc(T.sem.msa1, 1)
+    if uses_b:
+        V.memset(T.wb[:, 0:1024], 0.0).then_inc(T.sem.msb0, 1)
+        V.memset(T.wb[:, 1024:2048], 0.0).then_inc(T.sem.msb1, 1)
+        S.wait_ge(T.sem.msb0, 1)
+        for k in (2, 3):
+            S.activation(T.wb[:, 1024 * k:1024 * k + 1024], T.wb[:, 0:1024], COPY).then_inc(T.sem.ssb, 1)
     if rank in (1, 2):
         m, to = {1: (2, C[0]), 2: (3, C[1])}[rank]
         g.wait_ge(T.sem["m%da" % m], eng)
@@ -149,98 +178,110 @@ def rank_program(g, core, T, topo):
     if rank == 4:
         g.wait_ge(T.sem.lina, eng)
         n2 = _send(g, T, topo, core, [C[1]], "lin", T.lin[:], "lina", "sent2")
-    if rank in (0, 1, 2, 3):
+    if rank <= 4:
         consts_v()
-    if uses_b:
-        V.memset(T.wb[:], 0.0).then_inc(T.sem.ms3, 1)
-    if rank == 5:
-        V.wait_ge(T.sem.stl, 128)
-        v(V.tensor_scalar(T.sa[:], T.stw[:], 15, None, A.bitwise_and))
-        vw()
-        v(V.tensor_scalar(T.sa[:], T.sa[:], 4095, None, A.mult))
-        vw()
-        v(V.tensor_tensor(T.sa[:], T.sa[:], T.stw[:], A.add))
-        vw()
-        v(V.tensor_scalar(T.lin[:], T.sa[:], 0.0625, None, A.mult))
 
-    def windows(name):
-        todo = sorted((m, s) for m, w, s in steps if w == name)
-        if rank == 0 and name == "wa":
-            todo = todo[::-1]
+    ready = []
+
+    def window(m):
+        w, s = [(w, s) for mm, w, s in steps if mm == m][0]
+        x = w[1]
         for q, lo in ((Y, 0), (S, 4)):
-            if name == "wa":
-                q.wait_ge(T.sem.ms1, 1)
-                q.wait_ge(T.sem.ms2, 1)
-                q.wait_ge(T.sem.ssa, 2)
-            if name == "wb":
-                q.wait_ge(T.sem.ms3, 1)
-            if name == "w5":
-                q.wait_ge(T.sem.ms1, 1)
-                q.wait_ge(T.sem.gi, 1)
-            for m, s in todo:
-                if name != "w5":
-                    q.wait_ge(T.sem["m%da" % m], eng)
-                src = T.bp[:] if name == "w5" else T["m%d" % m][:]
-                for gr in range(lo, lo + 4):
-                    p = 16 * gr + s
-                    q.dma_start(T[name][p:p + 1, :], src).then_inc(T.sem[name + "l"], 16)
-        return 128 * len(todo)
+            if w not in ready:
+                q.wait_ge(T.sem["ms%s0" % x], 1)
+                q.wait_ge(T.sem["ms%s1" % x], 1)
+                q.wait_ge(T.sem["ss%s" % x], 2)
+            q.wait_ge(T.sem["m%da" % m], eng)
+            for gr in range(lo, lo + 4):
+                p = 16 * gr + s
+                q.dma_start(T[w][p:p + 1, :], T["m%d" % m][:]).then_inc(T.sem[w + "l"], 16)
+        ready.append(w)
 
-    need = {}
+    if rank == 0:
+        window(4)
+        window(3)
+        window(1)
+        window(2)
+        load_tab(S)
+    if rank == 1:
+        window(2)
+        window(4)
+        window(3)
+        load_tab(S)
+    if rank == 2:
+        Y.wait_ge(T.sem.sent, nsent)
+        load_tab(Y)
+        window(3)
+        Y.wait_ge(T.sem.sent2, n2)
+        load_tab(Y)
+    if rank == 3:
+        window(4)
+        load_tab(S)
+    if rank == 4:
+        Y.wait_ge(T.sem.sent, nsent)
+        load_tab(Y)
+        Y.wait_ge(T.sem.sent2, n2)
+        load_tab(Y)
     if rank == 5:
-        need["w5"] = ("w5l", windows("w5"))
-        load_tab(1)
         for q in range(8):
             S.dma_start(T.sto[16 * q:16 * q + 16, :], T.st[:]).then_inc(T.sem.sol, 16)
-        Y.wait_ge(T.sem.sent2, eng)
-        load_tab(2)
-    elif rank == 0:
-        need["wa"] = ("wal", windows("wa"))
-        need["wb"] = ("wbl", windows("wb"))
-    elif rank == 3:
-        need["wa"] = ("wal", windows("wa"))
-        Y.wait_ge(T.sem.sent, nsent)
-        load_tab(1)
-    else:
-        Y.wait_ge(T.sem.sent, nsent)
-        load_tab(1)
-        if uses_a:
-            need["wa"] = ("wal", windows("wa"))
-        if uses_b:
-            need["wb"] = ("wbl", windows("wb"))
 
-    if rank == 4:
-        V.wait_ge(T.sem.offa, eng)
-        S.wait_ge(T.sem.offa, eng)
+    if rank == 5:
+        V.wait_ge(T.sem.gq, gn[0])
+        v(V.tensor_scalar(T.bi[:], T.bi[:], 15, None, A.bitwise_and))
+        vw()
+        v(V.tensor_scalar(T.i16[:], T.bi[:], 0, None, A.is_equal))
+        V.wait_ge(T.sem.stl, 128)
+        v(V.tensor_scalar(T.sa[:], T.stw[:], 15, None, A.bitwise_and))
+        v(V.tensor_scalar(T.sb[:], T.stw[:], 4, None, A.logical_shift_right))
+        vw()
+        v(V.tensor_copy(T.lo[:], T.sa[:]))
+        v(V.tensor_copy(T.hi[:], T.sb[:]))
+        vw()
+        v(V.tensor_copy(T.mrow[:], T.i16[:, 0:16].indirect(T.lo[:, 0:8])))
+        V.wait_ge(T.sem.w5l, 128)
+        vw()
+        v(V.tensor_tensor(T.xm[:], T.w5[:, 0:256].indirect(T.hi[:, 0:8]), T.mrow[:], A.mult))
+        g.tensor.wait_ge(T.sem.vq, vn[0])
+        g.tensor.matmul(T.ps1[:, 0:8], T.xm[:], T.gs[:], True, True).then_inc(T.sem.pq, 1)
+        V.wait_ge(T.sem.pq, 1)
+        v(V.tensor_copy(T.lst[:], T.ps1[:, 0:8]))
+        g.wait_ge(T.sem.vq, vn[0])
+        n2 = _send(g, T, topo, core, [C[4], C[3], C[0]], "lin", T.lst[:], "lina", "sent2")
+        Y.wait_ge(T.sem.sent2, n2)
+        load_tab(Y)
+        V.wait_ge(T.sem.sol, 128)
+        v(V.tensor_copy(T.offs[:], T.sto[:]))
+    elif rank == 4:
+        V.wait_ge(T.sem.lina, eng)
+        v(V.tensor_scalar(T.l16[:], T.lin[:], 2048.0, None, A.subtract))
+        g.tensor.wait_ge(T.sem.vq, vn[0])
+        for G in range(8):
+            g.tensor.matmul(T.ps2[:, G::8], T.bg[:, 128 * G:128 * G + 128], T.l16[:], True, True).then_inc(T.sem.pq, 1)
+        V.wait_ge(T.sem.pq, 8)
+        v(V.tensor_scalar(T.offs[:], T.ps2[:], 2048.0, None, A.add))
     else:
         cur = T.lin
-        if rank != 5:
-            V.wait_ge(T.sem.lina, eng)
-        ready = []
+        V.wait_ge(T.sem.lina, eng)
+        got = []
         for k, (m, w, s) in enumerate(steps):
-            if w not in ready:
-                V.wait_ge(T.sem[need[w][0]], need[w][1])
-                ready.append(w)
+            if w not in got:
+                V.wait_ge(T.sem[w + "l"], 128 * len([1 for mm, ww, ss in steps if ww == w]))
+                got.append(w)
             vw()
             v(V.tensor_scalar(T.xr[:], T[w][:, 0:4096].indirect(cur[:, 0:8]), 2048.0, None, A.subtract))
             x_at = vn[0]
-            if k < len(steps) - 1 or rank in (3, 5):
+            if k < len(steps) - 1 or rank == 3:
                 vw()
                 v(V.transpose(T.xt[:], T.xr[:]))
                 vw()
                 v(V.tensor_scalar(T.lst[:], T.xt[:, s::16], 2048.0, None, A.add))
                 cur = T.lst
-                l_at = vn[0]
         if rank == 3:
-            g.wait_ge(T.sem.vq, l_at)
+            g.wait_ge(T.sem.vq, vn[0])
             n2 = _send(g, T, topo, core, [C[2]], "lin", T.lst[:], "lina", "sent2")
-        if rank == 5:
-            g.wait_ge(T.sem.vq, l_at)
-            n2 = _send(g, T, topo, core, [C[4], C[3], C[0]], "lin", T.lst[:], "lina", "sent2")
-            consts_g()
-            consts_v()
-            x_at = vn[0]
-        out = T.offx if rank == 5 else T.offs
+            Y.wait_ge(T.sem.sent2, n2)
+            load_tab(Y)
         g.tensor.wait_ge(T.sem.vq, x_at)
         g.tensor.matmul(T.ps1[:], T.xr[:], T.sel16[:], True, True).then_inc(T.sem.pq, 1)
         V.wait_ge(T.sem.pq, 1)
@@ -248,29 +289,22 @@ def rank_program(g, core, T, topo):
         g.tensor.wait_ge(T.sem.vq, vn[0])
         g.tensor.matmul(T.ps2[:], T.bt[:], T.ex[:], True, True).then_inc(T.sem.pq, 1)
         V.wait_ge(T.sem.pq, 2)
-        v(V.tensor_scalar(out[:], T.ps2[:], 2048.0, None, A.add))
-        if rank == 5:
-            g.wait_ge(T.sem.vq, vn[0])
-            n3 = _send(g, T, topo, core, [C[4]], "offs", T.offx[:], "offa", "sent3")
-            V.wait_ge(T.sem.sol, 128)
-            v(V.tensor_copy(T.offs[:], T.sto[:]))
-        vw()
-        S.wait_ge(T.sem.vq, vn[0])
+        v(V.tensor_scalar(T.offs[:], T.ps2[:], 2048.0, None, A.add))
+    vw()
+    S.wait_ge(T.sem.vq, vn[0])
 
-    V.wait_ge(T.sem.tabl, 16 * len(pieces))
-    v(V.tensor_copy(T.ysb[:, 0:512], T.tabs[:, 0:4096].indirect(T.offs[:, 0:32])))
-    S.wait_ge(T.sem.tabl, 16 * len(pieces))
-    S.activation(T.ysb[:, 512:1024], T.tabs[:, 0:4096].indirect(T.offs[:, 32:64]), ActivationFunctionType.Copy).then_inc(T.sem.sc, 1)
-    Y.wait_ge(T.sem.vq, vn[0])
-    Y.dma_start(T.y[:, 0:512], T.ysb[:, 0:512]).then_inc(T.sem.stq, 16)
+    npieces = len(TAB[rank])
+    V.wait_ge(T.sem.tabl, 16 * npieces)
+    S.wait_ge(T.sem.tabl, 16 * npieces)
+    for c in (0, 256):
+        v(V.tensor_copy(T.ysb[:, c:c + 256], T.tabs[:, 0:4096].indirect(T.offs[:, c // 16:c // 16 + 16])))
+        Y.wait_ge(T.sem.vq, vn[0])
+        Y.dma_start(T.y[:, c:c + 256], T.ysb[:, c:c + 256]).then_inc(T.sem.stq, 16)
+    S.activation(T.ysb[:, 512:1024], T.tabs[:, 0:4096].indirect(T.offs[:, 32:64]), COPY).then_inc(T.sem.sc, 1)
     S.wait_ge(T.sem.sc, 1)
     S.dma_start(T.y[:, 512:1024], T.ysb[:, 512:1024]).then_inc(T.sem.stq, 16)
-    Y.wait_ge(T.sem.stq, 32)
+    Y.wait_ge(T.sem.stq, 48)
     if 1 <= rank <= 4:
         g.wait_ge(T.sem.sent, nsent)
-    if rank >= 2:
+    if rank >= 1:
         g.wait_ge(T.sem.sent2, n2)
-    if rank == 1:
-        g.wait_ge(T.sem.sent2, n2)
-    if rank == 5:
-        g.wait_ge(T.sem.sent3, n3)

from concourse.bass import DstId, RemoteDMATransfer
from concourse.mybir import AluOpType, ActivationFunctionType

SCRATCH = {
    "tabs": ("sbuf", [128, 4096], "float32"),
    "wa": ("sbuf", [128, 4096], "float32"),
    "wb": ("sbuf", [128, 4096], "float32"),
    "w5": ("sbuf", [128, 256], "int32"),
    "ysb": ("sbuf", [128, 1024], "float32"),
    "raw": ("sbuf", [128, 64], "int32"),
    "x1": ("sbuf", [128, 32], "float32"),
    "nat": ("sbuf", [128, 32], "float32"),
    "stw": ("sbuf", [128, 8], "int32"),
    "sa": ("sbuf", [128, 8], "int32"),
    "sb": ("sbuf", [128, 8], "int32"),
    "lo": ("sbuf", [128, 8], "uint16"),
    "hi": ("sbuf", [128, 8], "uint16"),
    "i16": ("sbuf", [128, 16], "float32"),
    "mrow": ("sbuf", [128, 128], "float32"),
    "xm": ("sbuf", [128, 128], "float32"),
    "gs": ("sbuf", [128, 8], "float32"),
    "sto": ("sbuf", [128, 64], "int32"),
    "lin": ("sbuf", [128, 8], "uint16"),
    "lst": ("sbuf", [128, 8], "uint16"),
    "l16": ("sbuf", [128, 8], "float16"),
    "offs": ("sbuf", [128, 64], "uint16"),
    "xr": ("sbuf", [128, 128], "float16"),
    "xt": ("sbuf", [128, 128], "float16"),
    "ones": ("sbuf", [128, 64], "float32"),
    "sel": ("sbuf", [128, 64], "float32"),
    "mk": ("sbuf", [128, 64], "float32"),
    "bi": ("sbuf", [128, 16], "int32"),
    "sel16": ("sbuf", [128, 64], "float16"),
    "bt": ("sbuf", [128, 128], "float16"),
    "bg": ("sbuf", [128, 1024], "float16"),
    "ex": ("sbuf", [128, 64], "float16"),
    "ps1": ("psum", [128, 64], "float32"),
    "ps2": ("psum", [128, 64], "float32"),
    "m1": ("dram", [128, 32], "float32"),
    "m2": ("dram", [128, 32], "float32"),
    "m3": ("dram", [128, 32], "float32"),
    "m4": ("dram", [128, 32], "float32"),
}
SEMAPHORES = ["bpl", "stl", "sol", "tabl", "on", "msa0", "msa1", "msb0", "msb1", "ssa", "ssb", "gq", "vq", "pq", "sc", "sent",
              "sent2", "w5l", "m1a", "m2a", "m3a", "m4a", "lina", "wal", "wbl", "stq"]

STEPS = {0: [(4, "wa", 0), (3, "wa", 1), (2, "wb", 0), (1, "wb", 1)],
         1: [(4, "wa", 0), (3, "wb", 0), (2, "wa", 1)],
         2: [(3, "wa", 0)], 3: [(4, "wa", 0)], 4: [], 5: []}
SWAPS = {0: 0, 1: 0, 2: 1, 3: 0}
TAB = {0: [3584, 512], 1: [3072, 1024], 2: [2048, 576, 1472], 3: [2432, 1344, 320], 4: [2432, 896, 768], 5: [2176, 1920]}


def _send(g, T, topo, core, dsts, name, src, sem, local):
    mask = topo.mask(core, dsts[0])
    for d in dsts:
        mask &= topo.mask(core, d)
    ids = []
    for d in dsts:
        rid, pid = topo.addr(d, core)
        ids.append(DstId(rid=rid, pnc=pid))
    g.remote_dma_fused([RemoteDMATransfer(dst_ids=ids, dma_engine_mask=mask, remote_sem=T.sem[sem], srcs=[src],
                                          dsts=[T[name][:] for d in dsts], alu_op=0)], local_sem=T.sem[local])
    return bin(mask).count("1")


def rank_program(g, core, T, topo):
    rank = T.rank_of(core)
    if rank is None:
        return
    C = T.cores
    A = AluOpType
    COPY = ActivationFunctionType.Copy
    V, S, Y = g.vector, g.scalar, g.sync
    eng = bin(topo.mask(C[3], C[0])).count("1")
    steps = STEPS[rank]
    uses_b = rank in (0, 1)
    vn, gn, nt = [0], [0], [0]

    def v(ins):
        ins.then_inc(T.sem.vq, 1)
        vn[0] += 1

    def vw():
        if vn[0]:
            V.wait_ge(T.sem.vq, vn[0])

    def gc(ins):
        ins.then_inc(T.sem.gq, 1)
        gn[0] += 1

    def load_tab(q):
        k = nt[0]
        nt[0] += 1
        a = sum(TAB[rank][:k])
        b = a + TAB[rank][k]
        q.dma_start(T.tabs[:, a:b], T.tab[:, a:b]).then_inc(T.sem.tabl, 16)

    if 1 <= rank <= 4:
        for a in range(4):
            Y.dma_start(T.raw[32 * a:32 * a + 16, :], T.bp[:, 64 * a:64 * a + 64]).then_inc(T.sem.bpl, 16)
            S.dma_start(T.raw[32 * a + 16:32 * a + 32, 0:63], T.bp[:, 64 * a + 1:64 * a + 64]).then_inc(T.sem.bpl, 16)
    if rank == 5:
        for q in range(8):
            (Y if q % 2 else S).dma_start(T.stw[16 * q:16 * q + 16, :], T.st[:, 8 * q:8 * q + 8]).then_inc(T.sem.stl, 16)
        for q in range(8):
            (Y if q % 2 else S).dma_start(T.w5[16 * q:16 * q + 16, :], T.bp[:]).then_inc(T.sem.w5l, 16)
    load_tab(Y)

    parts = []
    if rank <= 3:
        slot = steps[-1][2]
        if (SWAPS[rank] + len(steps) - 1) % 2 == 0:
            parts = [(T.sel[:], T.mk[:], T.ones[:], [[0, 8], [16, 8]], [[16, 8], [0, 8]], 0)]
        else:
            parts = [(T.sel[:, h::2], T.mk[:, h::2], T.ones[:, 0:32], [[0, 4], [16, 2], [32, 4]],
                      [[32, 4], [0, 2], [0, 4]], 16 * h) for h in range(2)]

    V.memset(T.ones[:], 1.0).then_inc(T.sem.on, 1)
    g.wait_ge(T.sem.on, 1)
    gc(g.iota(T.bi[:], [[1, 16]], 128, -1))
    for sel, mk, one, gp, cp, base in parts:
        gc(g.affine_select(sel, one, gp, A.is_equal, 0.0, slot, -1))
        gc(g.affine_select(mk, one, [[-s, n] for s, n in cp], A.is_ge, 0.0, -base, 1))
    if rank >= 4:
        gc(g.affine_select(T.gs[:], T.ones[:, 0:8], [[-16, 8]], A.is_ge, 0.0, 0, 1))
        g.wait_ge(T.sem.gq, gn[0])
        gc(g.affine_select(T.gs[:], T.gs[:], [[16, 8]], A.is_ge, 0.0, 15, -1))

    def consts_g():
        if parts:
            g.wait_ge(T.sem.gq, gn[0])
        for sel, mk, one, gp, cp, base in parts:
            gc(g.affine_select(mk, mk, cp, A.is_ge, 0.0, base + 15, -1))

    def consts_v():
        V.wait_ge(T.sem.gq, gn[0])
        v(V.tensor_scalar(T.bi[:], T.bi[:], 15, None, A.bitwise_and))
        if rank <= 3:
            v(V.tensor_copy(T.sel16[:], T.sel[:]))
        vw()
        v(V.tensor_scalar(T.bt[:, 0:16], T.bi[:], 0, None, A.is_equal))
        for w in (16, 32, 64):
            vw()
            v(V.tensor_copy(T.bt[:, w:2 * w], T.bt[:, 0:w]))
        if rank == 4:
            vw()
            for G in range(8):
                v(V.tensor_scalar(T.bg[:, 128 * G:128 * G + 128], T.bt[:], T.gs[:, G:G + 1], None, A.mult))

    if rank <= 3:
        V.memset(T.wa[:, 0:1024], 0.0).then_inc(T.sem.msa0, 1)
        S.wait_ge(T.sem.msa0, 1)
        for k in (2, 3):
            S.activation(T.wa[:, 1024 * k:1024 * k + 1024], T.wa[:, 0:1024], COPY).then_inc(T.sem.ssa, 1)
    nsent, n2 = 0, 0
    if 1 <= rank <= 4:
        V.wait_ge(T.sem.bpl, 128)
        v(V.tensor_copy(T.x1[:], T.raw[:, 0:63:2]))
        vw()
        v(V.transpose(T.nat[:], T.x1[:]))
        g.wait_ge(T.sem.vq, vn[0])
        dsts = {4: [C[3], C[0], C[1]], 3: [C[2], C[0]], 2: [C[1]], 1: [C[0]]}[rank]
        nsent = _send(g, T, topo, core, dsts, "m%d" % rank, T.nat[:], "m%da" % rank, "sent")
    consts_g()
    if rank <= 3:
        V.memset(T.wa[:, 1024:2048], 0.0).then_inc(T.sem.msa1, 1)
    if uses_b:
        V.memset(T.wb[:, 0:1024], 0.0).then_inc(T.sem.msb0, 1)
        V.memset(T.wb[:, 1024:2048], 0.0).then_inc(T.sem.msb1, 1)
        S.wait_ge(T.sem.msb0, 1)
        for k in (2, 3):
            S.activation(T.wb[:, 1024 * k:1024 * k + 1024], T.wb[:, 0:1024], COPY).then_inc(T.sem.ssb, 1)
    if rank in (1, 2):
        m, to = {1: (2, C[0]), 2: (3, C[1])}[rank]
        g.wait_ge(T.sem["m%da" % m], eng)
        n2 = _send(g, T, topo, core, [to], "m%d" % m, T["m%d" % m][:], "m%da" % m, "sent2")
    if rank == 4:
        g.wait_ge(T.sem.lina, eng)
        n2 = _send(g, T, topo, core, [C[1]], "lin", T.lin[:], "lina", "sent2")
    if rank <= 4:
        consts_v()

    ready = []

    def window(m):
        w, s = [(w, s) for mm, w, s in steps if mm == m][0]
        x = w[1]
        for q, lo in ((Y, 0), (S, 4)):
            if w not in ready:
                q.wait_ge(T.sem["ms%s0" % x], 1)
                q.wait_ge(T.sem["ms%s1" % x], 1)
                q.wait_ge(T.sem["ss%s" % x], 2)
            q.wait_ge(T.sem["m%da" % m], eng)
            for gr in range(lo, lo + 4):
                p = 16 * gr + s
                q.dma_start(T[w][p:p + 1, :], T["m%d" % m][:]).then_inc(T.sem[w + "l"], 16)
        ready.append(w)

    if rank == 0:
        window(4)
        window(3)
        window(1)
        window(2)
        load_tab(S)
    if rank == 1:
        window(2)
        window(4)
        window(3)
        load_tab(S)
    if rank == 2:
        Y.wait_ge(T.sem.sent, nsent)
        load_tab(Y)
        window(3)
        Y.wait_ge(T.sem.sent2, n2)
        load_tab(Y)
    if rank == 3:
        window(4)
        load_tab(S)
    if rank == 4:
        Y.wait_ge(T.sem.sent, nsent)
        load_tab(Y)
        Y.wait_ge(T.sem.sent2, n2)
        load_tab(Y)
    if rank == 5:
        for q in range(8):
            S.dma_start(T.sto[16 * q:16 * q + 16, :], T.st[:]).then_inc(T.sem.sol, 16)

    if rank == 5:
        V.wait_ge(T.sem.gq, gn[0])
        v(V.tensor_scalar(T.bi[:], T.bi[:], 15, None, A.bitwise_and))
        vw()
        v(V.tensor_scalar(T.i16[:], T.bi[:], 0, None, A.is_equal))
        V.wait_ge(T.sem.stl, 128)
        v(V.tensor_scalar(T.sa[:], T.stw[:], 15, None, A.bitwise_and))
        v(V.tensor_scalar(T.sb[:], T.stw[:], 4, None, A.logical_shift_right))
        vw()
        v(V.tensor_copy(T.lo[:], T.sa[:]))
        v(V.tensor_copy(T.hi[:], T.sb[:]))
        vw()
        v(V.tensor_copy(T.mrow[:], T.i16[:, 0:16].indirect(T.lo[:, 0:8])))
        V.wait_ge(T.sem.w5l, 128)
        vw()
        v(V.tensor_tensor(T.xm[:], T.w5[:, 0:256].indirect(T.hi[:, 0:8]), T.mrow[:], A.mult))
        g.tensor.wait_ge(T.sem.vq, vn[0])
        g.tensor.matmul(T.ps1[:, 0:8], T.xm[:], T.gs[:], True, True).then_inc(T.sem.pq, 1)
        V.wait_ge(T.sem.pq, 1)
        v(V.tensor_copy(T.lst[:], T.ps1[:, 0:8]))
        g.wait_ge(T.sem.vq, vn[0])
        n2 = _send(g, T, topo, core, [C[4], C[3], C[0]], "lin", T.lst[:], "lina", "sent2")
        Y.wait_ge(T.sem.sent2, n2)
        load_tab(Y)
        V.wait_ge(T.sem.sol, 128)
        v(V.tensor_copy(T.offs[:], T.sto[:]))
    elif rank == 4:
        V.wait_ge(T.sem.lina, eng)
        v(V.tensor_scalar(T.l16[:], T.lin[:], 2048.0, None, A.subtract))
        g.tensor.wait_ge(T.sem.vq, vn[0])
        for G in range(8):
            g.tensor.matmul(T.ps2[:, G::8], T.bg[:, 128 * G:128 * G + 128], T.l16[:], True, True).then_inc(T.sem.pq, 1)
        V.wait_ge(T.sem.pq, 8)
        v(V.tensor_scalar(T.offs[:], T.ps2[:], 2048.0, None, A.add))
    else:
        cur = T.lin
        V.wait_ge(T.sem.lina, eng)
        got = []
        for k, (m, w, s) in enumerate(steps):
            if w not in got:
                V.wait_ge(T.sem[w + "l"], 128 * len([1 for mm, ww, ss in steps if ww == w]))
                got.append(w)
            vw()
            v(V.tensor_scalar(T.xr[:], T[w][:, 0:4096].indirect(cur[:, 0:8]), 2048.0, None, A.subtract))
            x_at = vn[0]
            if k < len(steps) - 1 or rank == 3:
                vw()
                v(V.transpose(T.xt[:], T.xr[:]))
                vw()
                v(V.tensor_scalar(T.lst[:], T.xt[:, s::16], 2048.0, None, A.add))
                cur = T.lst
        if rank == 3:
            g.wait_ge(T.sem.vq, vn[0])
            n2 = _send(g, T, topo, core, [C[2]], "lin", T.lst[:], "lina", "sent2")
            Y.wait_ge(T.sem.sent2, n2)
            load_tab(Y)
        g.tensor.wait_ge(T.sem.vq, x_at)
        g.tensor.matmul(T.ps1[:], T.xr[:], T.sel16[:], True, True).then_inc(T.sem.pq, 1)
        V.wait_ge(T.sem.pq, 1)
        v(V.tensor_tensor(T.ex[:], T.ps1[:], T.mk[:], A.mult))
        g.tensor.wait_ge(T.sem.vq, vn[0])
        g.tensor.matmul(T.ps2[:], T.bt[:], T.ex[:], True, True).then_inc(T.sem.pq, 1)
        V.wait_ge(T.sem.pq, 2)
        v(V.tensor_scalar(T.offs[:], T.ps2[:], 2048.0, None, A.add))
    vw()
    S.wait_ge(T.sem.vq, vn[0])

    npieces = len(TAB[rank])
    V.wait_ge(T.sem.tabl, 16 * npieces)
    S.wait_ge(T.sem.tabl, 16 * npieces)
    for c in (0, 256):
        v(V.tensor_copy(T.ysb[:, c:c + 256], T.tabs[:, 0:4096].indirect(T.offs[:, c // 16:c // 16 + 16])))
        Y.wait_ge(T.sem.vq, vn[0])
        Y.dma_start(T.y[:, c:c + 256], T.ysb[:, c:c + 256]).then_inc(T.sem.stq, 16)
    S.activation(T.ysb[:, 512:1024], T.tabs[:, 0:4096].indirect(T.offs[:, 32:64]), COPY).then_inc(T.sem.sc, 1)
    S.wait_ge(T.sem.sc, 1)
    S.dma_start(T.y[:, 512:1024], T.ysb[:, 512:1024]).then_inc(T.sem.stq, 16)
    Y.wait_ge(T.sem.stq, 48)
    if 1 <= rank <= 4:
        g.wait_ge(T.sem.sent, nsent)
    if rank >= 1:
        g.wait_ge(T.sem.sent2, n2)
